import numpy as np
import ml_dtypes


def mxq(x, axis, fmt="e4m3"):
    dtype, down = {"e4m3": (ml_dtypes.float8_e4m3fn, 7), "e5m2": (ml_dtypes.float8_e5m2, 14)}[fmt]
    v = np.moveaxis(np.asarray(x, np.float32).astype(ml_dtypes.bfloat16).astype(np.float64), axis, -1)
    blocks = v.reshape(v.shape[:-1] + (-1, 32))
    amax = np.abs(blocks).max(-1, keepdims=True)
    byte = np.maximum(np.where(amax > 0, np.frexp(amax)[1] - 1 + 127, 0) - down, 1)
    scale = np.exp2(byte - 127.0)
    codes = (blocks / scale).astype(np.float32).astype(dtype).astype(np.float64)
    return np.moveaxis((codes * scale).reshape(v.shape), -1, axis)


WIDE = False


def mx_kscale(k):
    if not WIDE:
        return np.ones(k)
    levels = np.array([10, -10, 5, -5, 0])
    if k % 512:
        return np.exp2(np.random.permutation(np.resize(levels, k // 32))).repeat(32)
    a = np.empty((k // 512, 16))
    for p in range(k // 512):
        a[p, :8] = np.random.permutation(np.resize(levels, 8))
        for g in range(8):
            far = levels[np.abs(levels - a[p, g]) >= 10]
            a[p, g + 8] = far[np.random.randint(len(far))]
    return np.exp2(a.ravel()).repeat(32)


def f64(x):
    return np.asarray(x).astype(np.float64)


def striped(idx):
    return np.tile(idx.reshape(-1, 16).T, (8, 1)).astype(np.uint16)


def unstriped(offs):
    return offs[:16].T.reshape(-1).astype(np.int64)


E2M1 = np.array([0.0, 0.5, 1.0, 1.5, 2.0, 3.0, 4.0, 6.0, -0.0, -0.5, -1.0, -1.5, -2.0, -3.0, -4.0, -6.0])


def pack_weight(w, fmt):
    k, n = w.shape
    w = f64(np.asarray(w, np.float32).astype(ml_dtypes.bfloat16)).reshape(k // 32, 32, n)
    amax = np.abs(w).max(1)
    if fmt == "e4m3":
        byte = np.frexp(amax)[1] - 1 + 127 - 7
    else:
        mant, ex = np.frexp(amax / 6.0)
        byte = np.where(mant > 0.5, ex, ex - 1) + 127
    byte = np.clip(np.where(amax > 0, byte, 1), 1, 254)
    scaled = (w * np.exp2(127.0 - byte)[:, None, :]).reshape(k, n).astype(np.float32)
    by_word = np.ascontiguousarray(scaled.reshape(k // 512, 128, 4, n).transpose(0, 1, 3, 2))
    if fmt == "e4m3":
        words = by_word.astype(ml_dtypes.float8_e4m3fn).view(np.uint8)
    else:
        c = by_word.astype(ml_dtypes.float4_e2m1fn).view(np.uint8) & 0xF
        words = (c[..., 0::2] | (c[..., 1::2] << 4)).reshape(k // 512, 128, 2 * n)
    return np.ascontiguousarray(words), np.ascontiguousarray(byte.astype(np.uint8).reshape(k // 512, 16, n))


def unpack_weight(words, scales, fmt):
    g, _, n = scales.shape
    words = np.ascontiguousarray(words).reshape(g, 128, n, -1)
    if fmt == "e4m3":
        vals = words.view(ml_dtypes.float8_e4m3fn).astype(np.float64)
    else:
        nib = np.empty((g, 128, n, 4), np.uint8)
        nib[..., 0::2] = words & 0xF
        nib[..., 1::2] = words >> 4
        vals = E2M1[nib]
    vals = vals * np.repeat(np.exp2(scales.astype(np.float64) - 127.0), 8, axis=1)[..., None]
    return vals.transpose(0, 1, 3, 2).reshape(g * 512, n)


def gelu(v):
    return 0.5 * v * (1.0 + np.tanh(np.sqrt(2.0 / np.pi) * (v + 0.044715 * v**3)))


def striped8(idx):
    return np.concatenate([v.reshape(-1, 16).T for v in idx]).astype(np.uint16)


def unstriped8(offs):
    return np.stack([offs[16 * g:16 * g + 16].T.reshape(-1) for g in range(8)]).astype(np.int64)


def runs(v, idx8):
    k = np.arange(v.shape[0])
    return v[k[:, None], idx8[k % 512 // 64]]


K, T, S, P, H, N = 1024, 2048, 1024, 512, 1024, 384

def setup_inputs():
    n = np.random.standard_normal
    s = mx_kscale(K)[:, None]
    u = mx_kscale(H)[:, None]
    d = {}
    d["tab_words"], d["tab_scales"] = pack_weight(n((K, T)) * s, "e4m3")
    d["offs"] = striped8(np.stack([np.random.permutation(T)[:S] for _ in range(8)]))
    d["pos1"] = striped(np.random.permutation(S)[:P])
    d["pos2"] = striped(np.random.permutation(S)[:P])
    d["w1"] = (n((K, H)) / s * u.T / K**0.5).astype(np.float32)
    d["b1"] = (0.7 * n(H) * u[:, 0]).astype(np.float32)
    d["w2_words"], d["w2_scales"] = pack_weight(n((K, H)) / s * u.T / K**0.5, "e2m1")
    d["b2"] = (0.5 * n(H) * u[:, 0]).astype(np.float32)
    d["w3"] = (n((H, N)) / u / H**0.5).astype(np.float32)
    d["w4_words"], d["w4_scales"] = pack_weight(0.6 * n((H, N)) / u**2 / H**0.5, "e4m3")
    d["level"] = n(N).astype(np.float32)
    return d

def reference(tab_words, tab_scales, offs, pos1, pos2, w1, b1, w2_words, w2_scales, b2, w3, w4_words, w4_scales, level):
    v = runs(unpack_weight(tab_words, tab_scales, "e4m3"), unstriped8(offs))
    w2 = unpack_weight(w2_words, w2_scales, "e2m1")
    w4 = unpack_weight(w4_words, w4_scales, "e4m3")
    up = (mxq(f64(w1), 0, "e4m3").T @ v) + f64(b1)[:, None]
    down = (w2.T @ v) + f64(b2)[:, None]
    dp = down[:, unstriped(pos2)]
    x = np.maximum(up[:, unstriped(pos1)], dp)
    e = np.square(dp)
    y1 = mxq(f64(w3), 0, "e4m3").T @ mxq(x, 0, "e4m3")
    y2 = w4.T @ mxq(e, 0, "e4m3")
    return y1 - y2 - f64(level)[:, None]

@@ -1,0 +1,286 @@
+from contextlib import ExitStack
+
+import concourse.mybir as mybir
+
+K, T, S, PAIRS, H, N = 1024, 2048, 1024, 512, 1024, 384
+FLOPS = 2 * (2 * K * H * S + 2 * H * N * PAIRS)
+
+F32 = mybir.dt.float32
+BF16 = mybir.dt.bfloat16
+I32 = mybir.dt.int32
+U32 = mybir.dt.uint32
+U16 = mybir.dt.uint16
+U8 = mybir.dt.uint8
+FP8X4 = mybir.dt.float8_e4m3fn_x4
+FP4X4 = mybir.dt.float4_e2m1fn_x4
+ACT = mybir.ActivationFunctionType
+ALU = mybir.AluOpType
+
+P = 128
+PACK = 4
+K_PASS = P * PACK
+BANK = 512
+QUAD = 32
+HALF = 256
+
+
+def tile_list_seepage_alarm_scores_kernel(
+    tc, tab_words, tab_scales, offs, pos1, pos2, w1, b1, w2_words, w2_scales, b2, w3, w4_words, w4_scales, level, out
+):
+    nc = tc.nc
+    passes = K // K_PASS
+    groups = H // K_PASS
+    n_tiles = N // P
+
+    with ExitStack() as ctx:
+        keep = ctx.enter_context(tc.tile_pool(name="keep", bufs=1))
+        ring = ctx.enter_context(tc.tile_pool(name="ring", bufs=16))
+        stage = ctx.enter_context(tc.tile_pool(name="stage", bufs=3))
+        psum = ctx.enter_context(tc.psum_pool(name="psum", bufs=8))
+
+        def kept(shape, dtype, name):
+            return keep.tile(shape, dtype, name=name, align_bytes=64)
+
+        def load_scale_rows(queue, plane, scales):
+            for d in range(P // QUAD):
+                queue.dma_start(
+                    out=plane[QUAD * d : QUAD * d + 4, :, 0 : scales.shape[2]].bitcast(I32),
+                    in_=scales[:, 4 * d : 4 * d + 4, :].rearrange("a r c -> r a c").bitcast(I32),
+                )
+
+        offs_sb = keep.tile([P, S // 16], U16, name="offs_sb")
+        pos1_sb = keep.tile([P, PAIRS // 16], U16, name="pos1_sb")
+        pos2_sb = keep.tile([P, PAIRS // 16], U16, name="pos2_sb")
+        level_sb = kept([P, n_tiles], F32, "level_sb")
+        with nc.allow_non_contiguous_dma(reason="one level a partition"):
+            nc.scalar.dma_start(out=level_sb[:], in_=level.rearrange("(c p) -> p c", p=P))
+        nc.sync.dma_start(offs_sb[:], offs)
+        nc.sync.dma_start(pos2_sb[:], pos2)
+        nc.sync.dma_start(pos1_sb[:], pos1)
+
+        tab_sc = kept([P, T], U8, "tab_sc")
+        nc.vector.memset(tab_sc[:].bitcast(I32), 0)
+        nc.scalar.dma_start(
+            out=tab_sc[0:P:4, :].bitcast(I32), in_=tab_scales.rearrange("a q t -> q a t").bitcast(I32)
+        )
+        neg_level = kept([P, n_tiles], F32, "neg_level")
+        nc.scalar.activation(neg_level[:], level_sb[:], ACT.Copy, scale=-1.0)
+
+        def load_w2(g):
+            raw = kept([P, passes, 2 * K_PASS], U8, "w2_raw%d" % g)
+            cols = w2_words[:, :, 2 * K_PASS * g : 2 * K_PASS * (g + 1)]
+            nc.sync.dma_start(out=raw[:].bitcast(I32), in_=cols.rearrange("a p c -> p a c").bitcast(I32))
+            return raw
+
+        w2_raw = [load_w2(0)]
+        w2_sc_raw = kept([P, passes, H], U8, "w2_sc_raw")
+        nc.gpsimd.memset(w2_sc_raw[:].bitcast(I32), 0)
+        load_scale_rows(nc.gpsimd, w2_sc_raw, w2_scales)
+        b2_sb = kept([P, groups, PACK], F32, "b2_sb")
+        nc.gpsimd.dma_start(out=b2_sb[:], in_=b2.rearrange("(g p t) -> p g t", p=P, t=PACK))
+        b1_sb = kept([P, groups, PACK], F32, "b1_sb")
+        nc.gpsimd.dma_start(out=b1_sb[:], in_=b1.rearrange("(g p t) -> p g t", p=P, t=PACK))
+
+        def staged(shape, dtype):
+            return stage.tile(shape, dtype, name="staged", align_bytes=64)
+
+        def load_tab(a):
+            words = staged([P, T], I32)
+            nc.sync.dma_start(out=words[:], in_=tab_words[a].rearrange("p t i -> p (t i)").bitcast(I32))
+            return words
+
+        def load_w1(a, g):
+            raw = staged([P, PACK, K_PASS], F32)
+            rows = w1[a * K_PASS : (a + 1) * K_PASS, g * K_PASS : (g + 1) * K_PASS]
+            nc.sync.dma_start(out=raw[:], in_=rows.rearrange("(p j) c -> p j c", j=PACK))
+            return raw
+
+        def load_w3(g):
+            raw = staged([P, PACK, N], F32)
+            nc.sync.dma_start(out=raw[:], in_=w3[g * K_PASS : (g + 1) * K_PASS, :].rearrange("(p j) n -> p j n", j=PACK))
+            return raw
+
+        tab = [load_tab(0)]
+        w1_raw = {(0, 0): load_w1(0, 0)}
+        tab.append(load_tab(1))
+        w2_raw.append(load_w2(1))
+
+        v_sc = kept([P, passes * S], U8, "v_sc")
+        nc.vector.memset(v_sc[:].bitcast(I32), 0)
+        picked_sc = kept([P, S], U8, "picked_sc")
+        nc.vector.tensor_copy(picked_sc[:], tab_sc[:].indirect(offs_sb[:]))
+        for d in range(P // QUAD):
+            nc.scalar.dma_start(
+                out=v_sc[QUAD * d : QUAD * d + 4, :].bitcast(I32),
+                in_=picked_sc[QUAD * d : QUAD * (d + 1) : 4, :].bitcast(I32),
+            )
+
+        w2_codes, w2_sc = [], []
+
+        def deal_w2(g):
+            codes = kept([P, passes, 2 * K_PASS], U8, "w2_codes%d" % g)
+            sc = kept([P, passes, K_PASS], U8, "w2_sc%d" % g)
+            cols = slice(g * K_PASS, (g + 1) * K_PASS)
+            nc.vector.tensor_copy(
+                codes[:].bitcast(U16).rearrange("p a (t m) -> p a t m", t=PACK),
+                w2_raw[g][:].bitcast(U16).rearrange("p a (m t) -> p a t m", t=PACK),
+            )
+            nc.vector.tensor_copy(
+                sc[:].rearrange("p a (t m) -> p a t m", t=PACK),
+                w2_sc_raw[:, :, cols].rearrange("p a (m t) -> p a t m", t=PACK),
+            )
+            w2_codes.append(codes)
+            w2_sc.append(sc)
+
+        deal_w2(0)
+        v = {}
+        for a in range(passes):
+            for h in range(S // BANK):
+                picked = kept([P, BANK], U32, "v%d%d" % (a, h))
+                entries = offs_sb[:, h * BANK // 16 : (h + 1) * BANK // 16]
+                nc.vector.tensor_copy(picked[:], tab[a][:].bitcast(U32).indirect(entries))
+                v[a, h] = picked
+
+        w1_codes, w1_sc = {}, {}
+
+        def quantize_w1(a, g):
+            grouped = kept([P, PACK * K_PASS], BF16, "w1_bf%d%d" % (a, g))
+            nc.scalar.activation(
+                grouped[:].rearrange("p (t m j) -> p m j t", t=PACK, j=PACK),
+                w1_raw[a, g][:].rearrange("p j (m t) -> p m j t", t=PACK),
+                ACT.Copy,
+            )
+            codes = kept([P, K_PASS], U32, "w1_codes%d%d" % (a, g))
+            sc = kept([P, K_PASS], U8, "w1_sc%d%d" % (a, g))
+            nc.vector.quantize_mx(out=codes[:].bitcast(FP8X4), scales=sc[:], in_=grouped[:])
+            w1_codes[a, g], w1_sc[a, g] = codes, sc
+
+        def first_stage(weights, bias, pos_sb, picked):
+            for t in range(PACK):
+                rows = ring.tile([P, S], F32, name="rows")
+                for h in range(S // BANK):
+                    acc = psum.tile([P, BANK], F32, name="acc")
+                    for a in range(passes):
+                        lhsT, lhsT_scale = weights(a, t)
+                        nc.tensor.matmul_mx(
+                            out=acc[:],
+                            lhsT=lhsT,
+                            lhsT_scale=lhsT_scale,
+                            rhs=v[a, h][:].bitcast(FP8X4),
+                            rhs_scale=v_sc[:, a * S + h * BANK : a * S + (h + 1) * BANK],
+                            start=(a == 0),
+                            stop=(a == passes - 1),
+                        )
+                    nc.scalar.activation(rows[:, h * BANK : (h + 1) * BANK], acc[:], ACT.Identity, bias=bias[:, t : t + 1])
+                nc.vector.tensor_copy(picked[:, t, :], rows[:].indirect(pos_sb[:]))
+
+        def woven(bf, h):
+            return bf[:].rearrange("p (c i t) -> p c t i", i=4, t=PACK)
+
+        def by_row(picked, h):
+            return picked[:, :, h * HALF : (h + 1) * HALF].rearrange("p t (c i) -> p c t i", i=4)
+
+        def quantize(bf, width, name):
+            codes = kept([P, width], U32, name + "_codes")
+            sc = kept([P, width], U8, name + "_sc")
+            nc.vector.quantize_mx(out=codes[:].bitcast(FP8X4), scales=sc[:], in_=bf[:])
+            return codes, sc
+
+        down, e_q, x_q = [], {}, {}
+        quantize_w1(0, 0)
+        deal_w2(1)
+        for a, g in ((1, 0), (0, 1), (1, 1)):
+            w1_raw[a, g] = load_w1(a, g)
+        w4_sc = w2_sc_raw
+        load_scale_rows(nc.sync, w4_sc, w4_scales)
+        for g in range(groups):
+            picked = kept([P, PACK, PAIRS], F32, "down%d" % g)
+            first_stage(
+                lambda a, t, g=g: (w2_codes[g][:, a, 2 * P * t : 2 * P * (t + 1)].bitcast(FP4X4), w2_sc[g][:, a, P * t : P * (t + 1)]),
+                b2_sb[:, g, :],
+                pos2_sb,
+                picked,
+            )
+            down.append(picked)
+            if g == 0:
+                for a, gg in ((1, 0), (0, 1), (1, 1)):
+                    quantize_w1(a, gg)
+
+        def squares(g):
+            e_bf = kept([P, PAIRS * PACK], BF16, "e_bf%d" % g)
+            nc.scalar.activation(
+                e_bf[:].rearrange("p (c i t) -> p c t i", i=4, t=PACK),
+                down[g][:].rearrange("p t (c i) -> p c t i", i=4),
+                ACT.Square,
+            )
+            e_q[g] = quantize(e_bf, PAIRS, "e%d" % g)
+
+        w3_bf = kept([P, groups * N * PACK], BF16, "w3_bf")
+        w3_codes = kept([P, groups * N], U32, "w3_codes")
+        w3_sc = kept([P, groups * N], U8, "w3_sc")
+
+        def quantize_w3():
+            for g in range(groups):
+                raw = load_w3(g)
+                nc.vector.tensor_scalar_mul(
+                    w3_bf[:, g * N * PACK : (g + 1) * N * PACK].rearrange("p (c i j) -> p c j i", i=4, j=PACK),
+                    raw[:].rearrange("p j (c i) -> p c j i", i=4),
+                    -1.0,
+                )
+            for lo, hi in ((0, 512), (512, groups * N)):
+                nc.vector.quantize_mx(
+                    out=w3_codes[:, lo:hi].bitcast(FP8X4), scales=w3_sc[:, lo:hi], in_=w3_bf[:, PACK * lo : PACK * hi]
+                )
+
+        def up_stage(g):
+            picked = kept([P, PACK, PAIRS], F32, "up%d" % g)
+            first_stage(
+                lambda a, t: (w1_codes[a, g][:, P * t : P * (t + 1)].bitcast(FP8X4), w1_sc[a, g][:, P * t : P * (t + 1)]),
+                b1_sb[:, g, :],
+                pos1_sb,
+                picked,
+            )
+            return picked
+
+        def maxima(g, picked):
+            for h in range(PAIRS // HALF):
+                x_bf = kept([P, HALF * PACK], BF16, "x_bf%d%d" % (g, h))
+                nc.vector.tensor_tensor(woven(x_bf, h), by_row(picked, h), by_row(down[g], h), ALU.max)
+                x_q[g, h] = quantize(x_bf, HALF, "x%d%d" % (g, h))
+
+        up0 = up_stage(0)
+        quantize_w3()
+        w4_codes = staged([P, groups, N], I32)
+        nc.sync.dma_start(out=w4_codes[:], in_=w4_words.rearrange("g p n i -> p g (n i)").bitcast(I32))
+        maxima(0, up0)
+        squares(0)
+        squares(1)
+        up1 = up_stage(1)
+        maxima(1, up1)
+
+        for h in range(PAIRS // HALF):
+            cols = slice(h * HALF, (h + 1) * HALF)
+            for c in range(n_tiles):
+                acc = psum.tile([P, BANK], F32, name="acc")
+                steps = []
+                for g in range(groups):
+                    steps.append((w4_codes[:, g, c * P : (c + 1) * P], w4_sc[:, g, c * P : (c + 1) * P], e_q[g][0][:, cols], e_q[g][1][:, cols]))
+                for g in range(groups):
+                    w_cols = slice(g * N + c * P, g * N + (c + 1) * P)
+                    steps.append((w3_codes[:, w_cols], w3_sc[:, w_cols], x_q[g, h][0][:], x_q[g, h][1][:]))
+                for i, (lhsT, lhsT_scale, rhs, rhs_scale) in enumerate(steps):
+                    nc.tensor.matmul_mx(
+                        out=acc[:, 0:HALF],
+                        lhsT=lhsT.bitcast(FP8X4),
+                        lhsT_scale=lhsT_scale,
+                        rhs=rhs.bitcast(FP8X4),
+                        rhs_scale=rhs_scale,
+                        start=(i == 0),
+                        stop=(i == len(steps) - 1),
+                    )
+                res = kept([P, HALF], F32, "res%d%d" % (h, c))
+                if c == 1:
+                    nc.vector.tensor_scalar(res[:], acc[:, 0:HALF], -1.0, neg_level[:, c : c + 1], ALU.mult, ALU.add)
+                else:
+                    nc.scalar.activation(res[:], acc[:, 0:HALF], ACT.Identity, bias=neg_level[:, c : c + 1], scale=-1.0)
+                nc.sync.dma_start(out=out[c * P : (c + 1) * P, cols], in_=res[:])

@@ -34,12 +34,15 @@ def tile_list_seepage_alarm_scores_kernel(
 
     with ExitStack() as ctx:
         keep = ctx.enter_context(tc.tile_pool(name="keep", bufs=1))
-        ring = ctx.enter_context(tc.tile_pool(name="ring", bufs=16))
-        stage = ctx.enter_context(tc.tile_pool(name="stage", bufs=3))
+        ring = ctx.enter_context(tc.tile_pool(name="ring", bufs=11))
+        stage = ctx.enter_context(tc.tile_pool(name="stage", bufs=5))
         psum = ctx.enter_context(tc.psum_pool(name="psum", bufs=8))
 
         def kept(shape, dtype, name):
             return keep.tile(shape, dtype, name=name, align_bytes=64)
+
+        def staged(shape, dtype):
+            return stage.tile(shape, dtype, name="staged", align_bytes=64)
 
         def load_scale_rows(queue, plane, scales):
             for d in range(P // QUAD):
@@ -48,23 +51,10 @@ def tile_list_seepage_alarm_scores_kernel(
                     in_=scales[:, 4 * d : 4 * d + 4, :].rearrange("a r c -> r a c").bitcast(I32),
                 )
 
-        offs_sb = keep.tile([P, S // 16], U16, name="offs_sb")
-        pos1_sb = keep.tile([P, PAIRS // 16], U16, name="pos1_sb")
-        pos2_sb = keep.tile([P, PAIRS // 16], U16, name="pos2_sb")
-        level_sb = kept([P, n_tiles], F32, "level_sb")
-        with nc.allow_non_contiguous_dma(reason="one level a partition"):
-            nc.scalar.dma_start(out=level_sb[:], in_=level.rearrange("(c p) -> p c", p=P))
-        nc.sync.dma_start(offs_sb[:], offs)
-        nc.sync.dma_start(pos2_sb[:], pos2)
-        nc.sync.dma_start(pos1_sb[:], pos1)
-
-        tab_sc = kept([P, T], U8, "tab_sc")
-        nc.vector.memset(tab_sc[:].bitcast(I32), 0)
-        nc.scalar.dma_start(
-            out=tab_sc[0:P:4, :].bitcast(I32), in_=tab_scales.rearrange("a q t -> q a t").bitcast(I32)
-        )
-        neg_level = kept([P, n_tiles], F32, "neg_level")
-        nc.scalar.activation(neg_level[:], level_sb[:], ACT.Copy, scale=-1.0)
+        def load_bias(vec, name):
+            sb = kept([P, groups, PACK], F32, name)
+            nc.sync.dma_start(out=sb[:], in_=vec.rearrange("(g p t) -> p g t", p=P, t=PACK))
+            return sb
 
         def load_w2(g):
             raw = kept([P, passes, 2 * K_PASS], U8, "w2_raw%d" % g)
@@ -72,41 +62,47 @@ def tile_list_seepage_alarm_scores_kernel(
             nc.sync.dma_start(out=raw[:].bitcast(I32), in_=cols.rearrange("a p c -> p a c").bitcast(I32))
             return raw
 
-        w2_raw = [load_w2(0)]
-        w2_sc_raw = kept([P, passes, H], U8, "w2_sc_raw")
-        nc.gpsimd.memset(w2_sc_raw[:].bitcast(I32), 0)
-        load_scale_rows(nc.gpsimd, w2_sc_raw, w2_scales)
-        b2_sb = kept([P, groups, PACK], F32, "b2_sb")
-        nc.gpsimd.dma_start(out=b2_sb[:], in_=b2.rearrange("(g p t) -> p g t", p=P, t=PACK))
-        b1_sb = kept([P, groups, PACK], F32, "b1_sb")
-        nc.gpsimd.dma_start(out=b1_sb[:], in_=b1.rearrange("(g p t) -> p g t", p=P, t=PACK))
-
-        def staged(shape, dtype):
-            return stage.tile(shape, dtype, name="staged", align_bytes=64)
-
-        def load_tab(a):
-            words = staged([P, T], I32)
+        def load_tab(a, words):
             nc.sync.dma_start(out=words[:], in_=tab_words[a].rearrange("p t i -> p (t i)").bitcast(I32))
             return words
 
-        def load_w1(a, g):
-            raw = staged([P, PACK, K_PASS], F32)
-            rows = w1[a * K_PASS : (a + 1) * K_PASS, g * K_PASS : (g + 1) * K_PASS]
+        def load_rows(weight, a, cols):
+            raw = staged([P, PACK, cols.stop - cols.start], F32)
+            rows = weight[a * K_PASS : (a + 1) * K_PASS, cols]
             nc.sync.dma_start(out=raw[:], in_=rows.rearrange("(p j) c -> p j c", j=PACK))
             return raw
 
-        def load_w3(g):
-            raw = staged([P, PACK, N], F32)
-            nc.sync.dma_start(out=raw[:], in_=w3[g * K_PASS : (g + 1) * K_PASS, :].rearrange("(p j) n -> p j n", j=PACK))
-            return raw
+        def load_w1(a, g):
+            return load_rows(w1, a, slice(g * K_PASS, (g + 1) * K_PASS))
 
-        tab = [load_tab(0)]
-        w1_raw = {(0, 0): load_w1(0, 0)}
-        tab.append(load_tab(1))
-        w2_raw.append(load_w2(1))
-
+        offs_sb = keep.tile([P, S // 16], U16, name="offs_sb")
+        pos1_sb = keep.tile([P, PAIRS // 16], U16, name="pos1_sb")
+        pos2_sb = keep.tile([P, PAIRS // 16], U16, name="pos2_sb")
+        tab_sc = kept([P, T], U8, "tab_sc")
+        scale_rows = kept([P, passes, H], U8, "scale_rows")
         v_sc = kept([P, passes * S], U8, "v_sc")
+        nc.gpsimd.memset(tab_sc[:].bitcast(I32), 0)
+        nc.gpsimd.memset(scale_rows[:].bitcast(I32), 0)
         nc.vector.memset(v_sc[:].bitcast(I32), 0)
+
+        nc.sync.dma_start(
+            out=tab_sc[0:P:4, :].bitcast(I32), in_=tab_scales.rearrange("a q t -> q a t").bitcast(I32)
+        )
+        nc.sync.dma_start(offs_sb[:], offs)
+        nc.sync.dma_start(pos2_sb[:], pos2)
+        load_scale_rows(nc.scalar, scale_rows, w2_scales)
+        w2_raw = [load_w2(0)]
+        tab = [load_tab(0, staged([P, T], I32))]
+        w1_first = load_rows(w1, 0, slice(0, K_PASS // 2))
+        tab.append(load_tab(1, kept([P, T], I32, "tab1")))
+        w1_raw = {(0, 0): [w1_first, load_rows(w1, 0, slice(K_PASS // 2, K_PASS))]}
+        b2_sb = load_bias(b2, "b2_sb")
+        w2_raw.append(load_w2(1))
+        for a, g in ((1, 0), (0, 1), (1, 1)):
+            w1_raw[a, g] = [load_w1(a, g)]
+        b1_sb = load_bias(b1, "b1_sb")
+        nc.sync.dma_start(pos1_sb[:], pos1)
+
         picked_sc = kept([P, S], U8, "picked_sc")
         nc.vector.tensor_copy(picked_sc[:], tab_sc[:].indirect(offs_sb[:]))
         for d in range(P // QUAD):
@@ -117,9 +113,9 @@ def tile_list_seepage_alarm_scores_kernel(
 
         w2_codes, w2_sc = [], []
 
-        def deal_w2(g):
+        def deal_w2(g, sc_name):
             codes = kept([P, passes, 2 * K_PASS], U8, "w2_codes%d" % g)
-            sc = kept([P, passes, K_PASS], U8, "w2_sc%d" % g)
+            sc = kept([P, passes, K_PASS], U8, sc_name)
             cols = slice(g * K_PASS, (g + 1) * K_PASS)
             nc.vector.tensor_copy(
                 codes[:].bitcast(U16).rearrange("p a (t m) -> p a t m", t=PACK),
@@ -127,12 +123,12 @@ def tile_list_seepage_alarm_scores_kernel(
             )
             nc.vector.tensor_copy(
                 sc[:].rearrange("p a (t m) -> p a t m", t=PACK),
-                w2_sc_raw[:, :, cols].rearrange("p a (m t) -> p a t m", t=PACK),
+                scale_rows[:, :, cols].rearrange("p a (m t) -> p a t m", t=PACK),
             )
             w2_codes.append(codes)
             w2_sc.append(sc)
 
-        deal_w2(0)
+        deal_w2(0, "w2_sc0")
         v = {}
         for a in range(passes):
             for h in range(S // BANK):
@@ -141,133 +137,143 @@ def tile_list_seepage_alarm_scores_kernel(
                 nc.vector.tensor_copy(picked[:], tab[a][:].bitcast(U32).indirect(entries))
                 v[a, h] = picked
 
-        w1_codes, w1_sc = {}, {}
-
-        def quantize_w1(a, g):
-            grouped = kept([P, PACK * K_PASS], BF16, "w1_bf%d%d" % (a, g))
-            nc.scalar.activation(
-                grouped[:].rearrange("p (t m j) -> p m j t", t=PACK, j=PACK),
-                w1_raw[a, g][:].rearrange("p j (m t) -> p m j t", t=PACK),
-                ACT.Copy,
-            )
-            codes = kept([P, K_PASS], U32, "w1_codes%d%d" % (a, g))
-            sc = kept([P, K_PASS], U8, "w1_sc%d%d" % (a, g))
-            nc.vector.quantize_mx(out=codes[:].bitcast(FP8X4), scales=sc[:], in_=grouped[:])
-            w1_codes[a, g], w1_sc[a, g] = codes, sc
-
-        def first_stage(weights, bias, pos_sb, picked):
-            for t in range(PACK):
-                rows = ring.tile([P, S], F32, name="rows")
-                for h in range(S // BANK):
-                    acc = psum.tile([P, BANK], F32, name="acc")
-                    for a in range(passes):
-                        lhsT, lhsT_scale = weights(a, t)
-                        nc.tensor.matmul_mx(
-                            out=acc[:],
-                            lhsT=lhsT,
-                            lhsT_scale=lhsT_scale,
-                            rhs=v[a, h][:].bitcast(FP8X4),
-                            rhs_scale=v_sc[:, a * S + h * BANK : a * S + (h + 1) * BANK],
-                            start=(a == 0),
-                            stop=(a == passes - 1),
-                        )
-                    nc.scalar.activation(rows[:, h * BANK : (h + 1) * BANK], acc[:], ACT.Identity, bias=bias[:, t : t + 1])
-                nc.vector.tensor_copy(picked[:, t, :], rows[:].indirect(pos_sb[:]))
-
-        def woven(bf, h):
-            return bf[:].rearrange("p (c i t) -> p c t i", i=4, t=PACK)
-
-        def by_row(picked, h):
-            return picked[:, :, h * HALF : (h + 1) * HALF].rearrange("p t (c i) -> p c t i", i=4)
-
         def quantize(bf, width, name):
             codes = kept([P, width], U32, name + "_codes")
             sc = kept([P, width], U8, name + "_sc")
             nc.vector.quantize_mx(out=codes[:].bitcast(FP8X4), scales=sc[:], in_=bf[:])
             return codes, sc
 
-        down, e_q, x_q = [], {}, {}
-        quantize_w1(0, 0)
-        deal_w2(1)
-        for a, g in ((1, 0), (0, 1), (1, 1)):
-            w1_raw[a, g] = load_w1(a, g)
-        w4_sc = w2_sc_raw
-        load_scale_rows(nc.sync, w4_sc, w4_scales)
-        for g in range(groups):
-            picked = kept([P, PACK, PAIRS], F32, "down%d" % g)
-            first_stage(
-                lambda a, t, g=g: (w2_codes[g][:, a, 2 * P * t : 2 * P * (t + 1)].bitcast(FP4X4), w2_sc[g][:, a, P * t : P * (t + 1)]),
-                b2_sb[:, g, :],
-                pos2_sb,
-                picked,
-            )
-            down.append(picked)
-            if g == 0:
-                for a, gg in ((1, 0), (0, 1), (1, 1)):
-                    quantize_w1(a, gg)
+        w1_q = {}
 
-        def squares(g):
-            e_bf = kept([P, PAIRS * PACK], BF16, "e_bf%d" % g)
-            nc.scalar.activation(
-                e_bf[:].rearrange("p (c i t) -> p c t i", i=4, t=PACK),
-                down[g][:].rearrange("p t (c i) -> p c t i", i=4),
-                ACT.Square,
+        def quantize_w1(a, g):
+            grouped = kept([P, PACK * K_PASS], BF16, "w1_bf%d%d" % (a, g))
+            cast = nc.vector.tensor_copy if (a, g) in ((1, 0),) else nc.scalar.copy
+            dst = grouped[:].rearrange("p (t m j) -> p m j t", t=PACK, j=PACK)
+            width = P // len(w1_raw[a, g])
+            for i, raw in enumerate(w1_raw[a, g]):
+                cast(dst[:, i * width : (i + 1) * width], raw[:].rearrange("p j (m t) -> p m j t", t=PACK))
+            w1_q[a, g] = quantize(grouped, K_PASS, "w1_%d%d" % (a, g))
+
+        def w2_slice(g, t, a):
+            return w2_codes[g][:, a, 2 * P * t : 2 * P * (t + 1)].bitcast(FP4X4), w2_sc[g][:, a, P * t : P * (t + 1)]
+
+        def w1_slice(g, t, a):
+            codes, sc = w1_q[a, g]
+            return codes[:, P * t : P * (t + 1)].bitcast(FP8X4), sc[:, P * t : P * (t + 1)]
+
+        def product(weights, bias, g, t, h, rows):
+            acc = psum.tile([P, BANK], F32, name="acc")
+            order = range(passes) if h == 0 else range(passes - 1, -1, -1)
+            for i, a in enumerate(order):
+                lhsT, lhsT_scale = weights(g, t, a)
+                nc.tensor.matmul_mx(
+                    out=acc[:],
+                    lhsT=lhsT,
+                    lhsT_scale=lhsT_scale,
+                    rhs=v[a, h][:].bitcast(FP8X4),
+                    rhs_scale=v_sc[:, a * S + h * BANK : a * S + (h + 1) * BANK],
+                    start=(i == 0),
+                    stop=(i == passes - 1),
+                )
+            nc.scalar.activation(rows[:, h * BANK : (h + 1) * BANK], acc[:], ACT.Identity, bias=bias[:, g, t : t + 1])
+
+        def rows_of(weights, bias, g, t):
+            rows = ring.tile([P, S], F32, name="rows")
+            for h in range(S // BANK):
+                product(weights, bias, g, t, h, rows)
+            return rows
+
+        def woven(bf):
+            return bf.rearrange("p (c i t) -> p c t i", i=2, t=PACK)
+
+        def by_pairs(planes):
+            return planes.rearrange("p t (c i) -> p c t i", i=2)
+
+        down = [kept([P, PACK, PAIRS], F32, "down%d" % g) for g in range(groups)]
+        up0 = kept([P, PACK, PAIRS], F32, "up0")
+        e_q, x_q = {}, {}
+
+        def down_slice(g, t):
+            nc.vector.tensor_copy(down[g][:, t, :], rows_of(w2_slice, b2_sb, g, t)[:].indirect(pos2_sb[:]))
+
+        def down_first():
+            all_rows = [ring.tile([P, S], F32, name="rows") for t in range(PACK)]
+            for t0 in range(0, PACK, 2):
+                for h in range(S // BANK):
+                    for t in (t0, t0 + 1):
+                        product(w2_slice, b2_sb, 0, t, h, all_rows[t])
+            for t in range(PACK):
+                nc.vector.tensor_copy(down[0][:, t, :], all_rows[t][:].indirect(pos2_sb[:]))
+
+        def up_slice(t):
+            nc.vector.tensor_copy(up0[:, t, :], rows_of(w1_slice, b1_sb, 0, t)[:].indirect(pos1_sb[:]))
+
+        def squares(g, h=None):
+            if h is None:
+                e_bf = kept([P, PAIRS * PACK], BF16, "e_bf%d" % g)
+                nc.scalar.activation(woven(e_bf[:]), by_pairs(down[g][:]), ACT.Square)
+                codes, sc = quantize(e_bf, PAIRS, "e%d" % g)
+                for hh in range(PAIRS // HALF):
+                    e_q[g, hh] = codes[:, hh * HALF : (hh + 1) * HALF], sc[:, hh * HALF : (hh + 1) * HALF]
+            else:
+                e_bf = kept([P, HALF * PACK], BF16, "e_bf%d%d" % (g, h))
+                nc.scalar.activation(woven(e_bf[:]), by_pairs(down[g][:, :, h * HALF : (h + 1) * HALF]), ACT.Square)
+                e_q[g, h] = quantize(e_bf, HALF, "e%d%d" % (g, h))
+
+        def maxima(g, h, up_half):
+            x_bf = kept([P, HALF * PACK], BF16, "x_bf%d%d" % (g, h))
+            nc.vector.tensor_tensor(
+                woven(x_bf[:]), by_pairs(up_half), by_pairs(down[g][:, :, h * HALF : (h + 1) * HALF]), ALU.max
             )
-            e_q[g] = quantize(e_bf, PAIRS, "e%d" % g)
+            x_q[g, h] = quantize(x_bf, HALF, "x%d%d" % (g, h))
+
+        def maxima0():
+            x_bf = kept([P, PAIRS * PACK], BF16, "x_bf0")
+            nc.vector.tensor_tensor(woven(x_bf[:]), by_pairs(up0[:]), by_pairs(down[0][:]), ALU.max)
+            codes, sc = quantize(x_bf, PAIRS, "x0")
+            for h in range(PAIRS // HALF):
+                x_q[0, h] = codes[:, h * HALF : (h + 1) * HALF], sc[:, h * HALF : (h + 1) * HALF]
 
         w3_bf = kept([P, groups * N * PACK], BF16, "w3_bf")
         w3_codes = kept([P, groups * N], U32, "w3_codes")
         w3_sc = kept([P, groups * N], U8, "w3_sc")
 
+        def cast_w3(g, on_scalar):
+            raw = load_rows(w3, g, slice(0, N))
+            dst = woven(w3_bf[:, g * N * PACK : (g + 1) * N * PACK])
+            if on_scalar:
+                nc.scalar.activation(dst, by_pairs(raw[:]), ACT.Copy, scale=-1.0)
+            else:
+                nc.vector.tensor_scalar_mul(dst, by_pairs(raw[:]), -1.0)
+
         def quantize_w3():
-            for g in range(groups):
-                raw = load_w3(g)
-                nc.vector.tensor_scalar_mul(
-                    w3_bf[:, g * N * PACK : (g + 1) * N * PACK].rearrange("p (c i j) -> p c j i", i=4, j=PACK),
-                    raw[:].rearrange("p j (c i) -> p c j i", i=4),
-                    -1.0,
-                )
             for lo, hi in ((0, 512), (512, groups * N)):
                 nc.vector.quantize_mx(
                     out=w3_codes[:, lo:hi].bitcast(FP8X4), scales=w3_sc[:, lo:hi], in_=w3_bf[:, PACK * lo : PACK * hi]
                 )
 
-        def up_stage(g):
-            picked = kept([P, PACK, PAIRS], F32, "up%d" % g)
-            first_stage(
-                lambda a, t: (w1_codes[a, g][:, P * t : P * (t + 1)].bitcast(FP8X4), w1_sc[a, g][:, P * t : P * (t + 1)]),
-                b1_sb[:, g, :],
-                pos1_sb,
-                picked,
-            )
-            return picked
+        def load_last():
+            load_scale_rows(nc.sync, scale_rows, w4_scales)
+            codes = kept([P, groups, N], I32, "w4_codes")
+            nc.sync.dma_start(out=codes[:], in_=w4_words.rearrange("g p n i -> p g (n i)").bitcast(I32))
+            level_sb = kept([P, n_tiles], F32, "level_sb")
+            with nc.allow_non_contiguous_dma(reason="one level a partition"):
+                nc.sync.dma_start(out=level_sb[:], in_=level.rearrange("(c p) -> p c", p=P))
+            neg = kept([P, n_tiles], F32, "neg_level")
+            nc.vector.tensor_scalar_mul(neg[:], level_sb[:], -1.0)
+            return codes, neg
 
-        def maxima(g, picked):
-            for h in range(PAIRS // HALF):
-                x_bf = kept([P, HALF * PACK], BF16, "x_bf%d%d" % (g, h))
-                nc.vector.tensor_tensor(woven(x_bf, h), by_row(picked, h), by_row(down[g], h), ALU.max)
-                x_q[g, h] = quantize(x_bf, HALF, "x%d%d" % (g, h))
-
-        up0 = up_stage(0)
-        quantize_w3()
-        w4_codes = staged([P, groups, N], I32)
-        nc.sync.dma_start(out=w4_codes[:], in_=w4_words.rearrange("g p n i -> p g (n i)").bitcast(I32))
-        maxima(0, up0)
-        squares(0)
-        squares(1)
-        up1 = up_stage(1)
-        maxima(1, up1)
-
-        for h in range(PAIRS // HALF):
+        def scores(h):
             cols = slice(h * HALF, (h + 1) * HALF)
             for c in range(n_tiles):
                 acc = psum.tile([P, BANK], F32, name="acc")
                 steps = []
                 for g in range(groups):
-                    steps.append((w4_codes[:, g, c * P : (c + 1) * P], w4_sc[:, g, c * P : (c + 1) * P], e_q[g][0][:, cols], e_q[g][1][:, cols]))
+                    steps.append((w4_codes[:, g, c * P : (c + 1) * P], scale_rows[:, g, c * P : (c + 1) * P], e_q[g, h][0][:], e_q[g, h][1][:]))
                 for g in range(groups):
                     w_cols = slice(g * N + c * P, g * N + (c + 1) * P)
                     steps.append((w3_codes[:, w_cols], w3_sc[:, w_cols], x_q[g, h][0][:], x_q[g, h][1][:]))
+                steps = [steps[2], steps[0], steps[1], steps[3]]
                 for i, (lhsT, lhsT_scale, rhs, rhs_scale) in enumerate(steps):
                     nc.tensor.matmul_mx(
                         out=acc[:, 0:HALF],
@@ -279,8 +285,41 @@ def tile_list_seepage_alarm_scores_kernel(
                         stop=(i == len(steps) - 1),
                     )
                 res = kept([P, HALF], F32, "res%d%d" % (h, c))
-                if c == 1:
+                if h == 1 and c == 1:
                     nc.vector.tensor_scalar(res[:], acc[:, 0:HALF], -1.0, neg_level[:, c : c + 1], ALU.mult, ALU.add)
                 else:
                     nc.scalar.activation(res[:], acc[:, 0:HALF], ACT.Identity, bias=neg_level[:, c : c + 1], scale=-1.0)
                 nc.sync.dma_start(out=out[c * P : (c + 1) * P, cols], in_=res[:])
+
+        def last_halves(rows):
+            for h in range(PAIRS // HALF):
+                half = kept([P, PACK, HALF], F32, "up1_half")
+                entries = pos1_sb[:, h * HALF // 16 : (h + 1) * HALF // 16]
+                for t in range(PACK):
+                    nc.vector.tensor_copy(half[:, t, :], rows[t][:].indirect(entries))
+                maxima(1, h, half[:])
+                scores(h)
+
+        quantize_w1(0, 0)
+        deal_w2(1, "tab1")
+        down_first()
+        quantize_w1(1, 0)
+        for t in range(PACK):
+            down_slice(1, t)
+        quantize_w1(0, 1)
+        for t in range(2):
+            up_slice(t)
+        quantize_w1(1, 1)
+        up_slice(2)
+        up_slice(3)
+        w4_codes, neg_level = load_last()
+        cast_w3(0, True)
+        maxima0()
+        rows1 = [rows_of(w1_slice, b1_sb, 1, t) for t in range(PACK)]
+        cast_w3(1, True)
+        quantize_w3()
+        squares(0, 0)
+        squares(1, 0)
+        squares(0, 1)
+        squares(1, 1)
+        last_halves(rows1)

@@ -56,10 +56,10 @@ def tile_list_seepage_alarm_scores_kernel(
             nc.sync.dma_start(out=sb[:], in_=vec.rearrange("(g p t) -> p g t", p=P, t=PACK))
             return sb
 
-        def load_w2(g):
+        def load_w2(g, queue):
             raw = kept([P, passes, 2 * K_PASS], U8, "w2_raw%d" % g)
             cols = w2_words[:, :, 2 * K_PASS * g : 2 * K_PASS * (g + 1)]
-            nc.sync.dma_start(out=raw[:].bitcast(I32), in_=cols.rearrange("a p c -> p a c").bitcast(I32))
+            queue.dma_start(out=raw[:].bitcast(I32), in_=cols.rearrange("a p c -> p a c").bitcast(I32))
             return raw
 
         def load_tab(a, words):
@@ -81,23 +81,23 @@ def tile_list_seepage_alarm_scores_kernel(
         tab_sc = kept([P, T], U8, "tab_sc")
         scale_rows = kept([P, passes, H], U8, "scale_rows")
         v_sc = kept([P, passes * S], U8, "v_sc")
-        nc.gpsimd.memset(tab_sc[:].bitcast(I32), 0)
+        nc.vector.memset(tab_sc[:].bitcast(I32), 0)
         nc.gpsimd.memset(scale_rows[:].bitcast(I32), 0)
-        nc.vector.memset(v_sc[:].bitcast(I32), 0)
+        nc.gpsimd.memset(v_sc[:].bitcast(I32), 0)
 
         nc.sync.dma_start(
             out=tab_sc[0:P:4, :].bitcast(I32), in_=tab_scales.rearrange("a q t -> q a t").bitcast(I32)
         )
         nc.sync.dma_start(offs_sb[:], offs)
-        nc.sync.dma_start(pos2_sb[:], pos2)
+        w2_raw = [load_w2(0, nc.scalar)]
         load_scale_rows(nc.scalar, scale_rows, w2_scales)
-        w2_raw = [load_w2(0)]
         tab = [load_tab(0, staged([P, T], I32))]
-        w1_first = load_rows(w1, 0, slice(0, K_PASS // 2))
         tab.append(load_tab(1, kept([P, T], I32, "tab1")))
+        w1_first = load_rows(w1, 0, slice(0, K_PASS // 2))
         w1_raw = {(0, 0): [w1_first, load_rows(w1, 0, slice(K_PASS // 2, K_PASS))]}
         b2_sb = load_bias(b2, "b2_sb")
-        w2_raw.append(load_w2(1))
+        w2_raw.append(load_w2(1, nc.sync))
+        nc.sync.dma_start(pos2_sb[:], pos2)
         for a, g in ((1, 0), (0, 1), (1, 1)):
             w1_raw[a, g] = [load_w1(a, g)]
         b1_sb = load_bias(b1, "b1_sb")
@@ -163,7 +163,7 @@ def tile_list_seepage_alarm_scores_kernel(
 
         def product(weights, bias, g, t, h, rows):
             acc = psum.tile([P, BANK], F32, name="acc")
-            order = range(passes) if h == 0 else range(passes - 1, -1, -1)
+            order = range(passes) if h == 0 and t < 2 else range(passes - 1, -1, -1)
             for i, a in enumerate(order):
                 lhsT, lhsT_scale = weights(g, t, a)
                 nc.tensor.matmul_mx(

from contextlib import ExitStack

import concourse.mybir as mybir

K, T, S, PAIRS, H, N = 1024, 2048, 1024, 512, 1024, 384
FLOPS = 2 * (2 * K * H * S + 2 * H * N * PAIRS)

F32 = mybir.dt.float32
BF16 = mybir.dt.bfloat16
I32 = mybir.dt.int32
U32 = mybir.dt.uint32
U16 = mybir.dt.uint16
U8 = mybir.dt.uint8
FP8X4 = mybir.dt.float8_e4m3fn_x4
FP4X4 = mybir.dt.float4_e2m1fn_x4
ACT = mybir.ActivationFunctionType
ALU = mybir.AluOpType

P = 128
PACK = 4
K_PASS = P * PACK
BANK = 512
QUAD = 32
HALF = 256


def tile_list_seepage_alarm_scores_kernel(
    tc, tab_words, tab_scales, offs, pos1, pos2, w1, b1, w2_words, w2_scales, b2, w3, w4_words, w4_scales, level, out
):
    nc = tc.nc
    passes = K // K_PASS
    groups = H // K_PASS
    n_tiles = N // P

    with ExitStack() as ctx:
        keep = ctx.enter_context(tc.tile_pool(name="keep", bufs=1))
        ring = ctx.enter_context(tc.tile_pool(name="ring", bufs=11))
        stage = ctx.enter_context(tc.tile_pool(name="stage", bufs=5))
        psum = ctx.enter_context(tc.psum_pool(name="psum", bufs=8))

        def kept(shape, dtype, name):
            return keep.tile(shape, dtype, name=name, align_bytes=64)

        def staged(shape, dtype):
            return stage.tile(shape, dtype, name="staged", align_bytes=64)

        def load_scale_rows(queue, plane, scales):
            for d in range(P // QUAD):
                queue.dma_start(
                    out=plane[QUAD * d : QUAD * d + 4, :, 0 : scales.shape[2]].bitcast(I32),
                    in_=scales[:, 4 * d : 4 * d + 4, :].rearrange("a r c -> r a c").bitcast(I32),
                )

        def load_bias(vec, name):
            sb = kept([P, groups, PACK], F32, name)
            nc.sync.dma_start(out=sb[:], in_=vec.rearrange("(g p t) -> p g t", p=P, t=PACK))
            return sb

        def load_w2(g, queue):
            raw = kept([P, passes, 2 * K_PASS], U8, "w2_raw%d" % g)
            cols = w2_words[:, :, 2 * K_PASS * g : 2 * K_PASS * (g + 1)]
            queue.dma_start(out=raw[:].bitcast(I32), in_=cols.rearrange("a p c -> p a c").bitcast(I32))
            return raw

        def load_tab(a, words):
            nc.sync.dma_start(out=words[:], in_=tab_words[a].rearrange("p t i -> p (t i)").bitcast(I32))
            return words

        def load_rows(weight, a, cols):
            raw = staged([P, PACK, cols.stop - cols.start], F32)
            rows = weight[a * K_PASS : (a + 1) * K_PASS, cols]
            nc.sync.dma_start(out=raw[:], in_=rows.rearrange("(p j) c -> p j c", j=PACK))
            return raw

        def load_w1(a, g):
            return load_rows(w1, a, slice(g * K_PASS, (g + 1) * K_PASS))

        offs_sb = keep.tile([P, S // 16], U16, name="offs_sb")
        pos1_sb = keep.tile([P, PAIRS // 16], U16, name="pos1_sb")
        pos2_sb = keep.tile([P, PAIRS // 16], U16, name="pos2_sb")
        tab_sc = kept([P, T], U8, "tab_sc")
        scale_rows = kept([P, passes, H], U8, "scale_rows")
        v_sc = kept([P, passes * S], U8, "v_sc")
        nc.vector.memset(tab_sc[:].bitcast(I32), 0)
        nc.gpsimd.memset(scale_rows[:].bitcast(I32), 0)
        nc.gpsimd.memset(v_sc[:].bitcast(I32), 0)

        nc.sync.dma_start(
            out=tab_sc[0:P:4, :].bitcast(I32), in_=tab_scales.rearrange("a q t -> q a t").bitcast(I32)
        )
        nc.sync.dma_start(offs_sb[:], offs)
        w2_raw = [load_w2(0, nc.scalar)]
        load_scale_rows(nc.scalar, scale_rows, w2_scales)
        tab = [load_tab(0, staged([P, T], I32))]
        tab.append(load_tab(1, kept([P, T], I32, "tab1")))
        w1_first = load_rows(w1, 0, slice(0, K_PASS // 2))
        w1_raw = {(0, 0): [w1_first, load_rows(w1, 0, slice(K_PASS // 2, K_PASS))]}
        b2_sb = load_bias(b2, "b2_sb")
        w2_raw.append(load_w2(1, nc.sync))
        nc.sync.dma_start(pos2_sb[:], pos2)
        for a, g in ((1, 0), (0, 1), (1, 1)):
            w1_raw[a, g] = [load_w1(a, g)]
        b1_sb = load_bias(b1, "b1_sb")
        nc.sync.dma_start(pos1_sb[:], pos1)

        picked_sc = kept([P, S], U8, "picked_sc")
        nc.vector.tensor_copy(picked_sc[:], tab_sc[:].indirect(offs_sb[:]))
        for d in range(P // QUAD):
            nc.scalar.dma_start(
                out=v_sc[QUAD * d : QUAD * d + 4, :].bitcast(I32),
                in_=picked_sc[QUAD * d : QUAD * (d + 1) : 4, :].bitcast(I32),
            )

        w2_codes, w2_sc = [], []

        def deal_w2(g, sc_name):
            codes = kept([P, passes, 2 * K_PASS], U8, "w2_codes%d" % g)
            sc = kept([P, passes, K_PASS], U8, sc_name)
            cols = slice(g * K_PASS, (g + 1) * K_PASS)
            nc.vector.tensor_copy(
                codes[:].bitcast(U16).rearrange("p a (t m) -> p a t m", t=PACK),
                w2_raw[g][:].bitcast(U16).rearrange("p a (m t) -> p a t m", t=PACK),
            )
            nc.vector.tensor_copy(
                sc[:].rearrange("p a (t m) -> p a t m", t=PACK),
                scale_rows[:, :, cols].rearrange("p a (m t) -> p a t m", t=PACK),
            )
            w2_codes.append(codes)
            w2_sc.append(sc)

        deal_w2(0, "w2_sc0")
        v = {}
        for a in range(passes):
            for h in range(S // BANK):
                picked = kept([P, BANK], U32, "v%d%d" % (a, h))
                entries = offs_sb[:, h * BANK // 16 : (h + 1) * BANK // 16]
                nc.vector.tensor_copy(picked[:], tab[a][:].bitcast(U32).indirect(entries))
                v[a, h] = picked

        def quantize(bf, width, name):
            codes = kept([P, width], U32, name + "_codes")
            sc = kept([P, width], U8, name + "_sc")
            nc.vector.quantize_mx(out=codes[:].bitcast(FP8X4), scales=sc[:], in_=bf[:])
            return codes, sc

        w1_q = {}

        def quantize_w1(a, g):
            grouped = kept([P, PACK * K_PASS], BF16, "w1_bf%d%d" % (a, g))
            cast = nc.vector.tensor_copy if (a, g) in ((1, 0),) else nc.scalar.copy
            dst = grouped[:].rearrange("p (t m j) -> p m j t", t=PACK, j=PACK)
            width = P // len(w1_raw[a, g])
            for i, raw in enumerate(w1_raw[a, g]):
                cast(dst[:, i * width : (i + 1) * width], raw[:].rearrange("p j (m t) -> p m j t", t=PACK))
            w1_q[a, g] = quantize(grouped, K_PASS, "w1_%d%d" % (a, g))

        def w2_slice(g, t, a):
            return w2_codes[g][:, a, 2 * P * t : 2 * P * (t + 1)].bitcast(FP4X4), w2_sc[g][:, a, P * t : P * (t + 1)]

        def w1_slice(g, t, a):
            codes, sc = w1_q[a, g]
            return codes[:, P * t : P * (t + 1)].bitcast(FP8X4), sc[:, P * t : P * (t + 1)]

        def product(weights, bias, g, t, h, rows):
            acc = psum.tile([P, BANK], F32, name="acc")
            order = range(passes) if h == 0 and t < 2 else range(passes - 1, -1, -1)
            for i, a in enumerate(order):
                lhsT, lhsT_scale = weights(g, t, a)
                nc.tensor.matmul_mx(
                    out=acc[:],
                    lhsT=lhsT,
                    lhsT_scale=lhsT_scale,
                    rhs=v[a, h][:].bitcast(FP8X4),
                    rhs_scale=v_sc[:, a * S + h * BANK : a * S + (h + 1) * BANK],
                    start=(i == 0),
                    stop=(i == passes - 1),
                )
            nc.scalar.activation(rows[:, h * BANK : (h + 1) * BANK], acc[:], ACT.Identity, bias=bias[:, g, t : t + 1])

        def rows_of(weights, bias, g, t):
            rows = ring.tile([P, S], F32, name="rows")
            for h in range(S // BANK):
                product(weights, bias, g, t, h, rows)
            return rows

        def woven(bf):
            return bf.rearrange("p (c i t) -> p c t i", i=2, t=PACK)

        def by_pairs(planes):
            return planes.rearrange("p t (c i) -> p c t i", i=2)

        down = [kept([P, PACK, PAIRS], F32, "down%d" % g) for g in range(groups)]
        up0 = kept([P, PACK, PAIRS], F32, "up0")
        e_q, x_q = {}, {}

        def down_slice(g, t):
            nc.vector.tensor_copy(down[g][:, t, :], rows_of(w2_slice, b2_sb, g, t)[:].indirect(pos2_sb[:]))

        def down_first():
            all_rows = [ring.tile([P, S], F32, name="rows") for t in range(PACK)]
            for t0 in range(0, PACK, 2):
                for h in range(S // BANK):
                    for t in (t0, t0 + 1):
                        product(w2_slice, b2_sb, 0, t, h, all_rows[t])
            for t in range(PACK):
                nc.vector.tensor_copy(down[0][:, t, :], all_rows[t][:].indirect(pos2_sb[:]))

        def up_slice(t):
            nc.vector.tensor_copy(up0[:, t, :], rows_of(w1_slice, b1_sb, 0, t)[:].indirect(pos1_sb[:]))

        def squares(g, h=None):
            if h is None:
                e_bf = kept([P, PAIRS * PACK], BF16, "e_bf%d" % g)
                nc.scalar.activation(woven(e_bf[:]), by_pairs(down[g][:]), ACT.Square)
                codes, sc = quantize(e_bf, PAIRS, "e%d" % g)
                for hh in range(PAIRS // HALF):
                    e_q[g, hh] = codes[:, hh * HALF : (hh + 1) * HALF], sc[:, hh * HALF : (hh + 1) * HALF]
            else:
                e_bf = kept([P, HALF * PACK], BF16, "e_bf%d%d" % (g, h))
                nc.scalar.activation(woven(e_bf[:]), by_pairs(down[g][:, :, h * HALF : (h + 1) * HALF]), ACT.Square)
                e_q[g, h] = quantize(e_bf, HALF, "e%d%d" % (g, h))

        def maxima(g, h, up_half):
            x_bf = kept([P, HALF * PACK], BF16, "x_bf%d%d" % (g, h))
            nc.vector.tensor_tensor(
                woven(x_bf[:]), by_pairs(up_half), by_pairs(down[g][:, :, h * HALF : (h + 1) * HALF]), ALU.max
            )
            x_q[g, h] = quantize(x_bf, HALF, "x%d%d" % (g, h))

        def maxima0():
            x_bf = kept([P, PAIRS * PACK], BF16, "x_bf0")
            nc.vector.tensor_tensor(woven(x_bf[:]), by_pairs(up0[:]), by_pairs(down[0][:]), ALU.max)
            codes, sc = quantize(x_bf, PAIRS, "x0")
            for h in range(PAIRS // HALF):
                x_q[0, h] = codes[:, h * HALF : (h + 1) * HALF], sc[:, h * HALF : (h + 1) * HALF]

        w3_bf = kept([P, groups * N * PACK], BF16, "w3_bf")
        w3_codes = kept([P, groups * N], U32, "w3_codes")
        w3_sc = kept([P, groups * N], U8, "w3_sc")

        def cast_w3(g, on_scalar):
            raw = load_rows(w3, g, slice(0, N))
            dst = woven(w3_bf[:, g * N * PACK : (g + 1) * N * PACK])
            if on_scalar:
                nc.scalar.activation(dst, by_pairs(raw[:]), ACT.Copy, scale=-1.0)
            else:
                nc.vector.tensor_scalar_mul(dst, by_pairs(raw[:]), -1.0)

        def quantize_w3():
            for lo, hi in ((0, 512), (512, groups * N)):
                nc.vector.quantize_mx(
                    out=w3_codes[:, lo:hi].bitcast(FP8X4), scales=w3_sc[:, lo:hi], in_=w3_bf[:, PACK * lo : PACK * hi]
                )

        def load_last():
            load_scale_rows(nc.sync, scale_rows, w4_scales)
            codes = kept([P, groups, N], I32, "w4_codes")
            nc.sync.dma_start(out=codes[:], in_=w4_words.rearrange("g p n i -> p g (n i)").bitcast(I32))
            level_sb = kept([P, n_tiles], F32, "level_sb")
            with nc.allow_non_contiguous_dma(reason="one level a partition"):
                nc.sync.dma_start(out=level_sb[:], in_=level.rearrange("(c p) -> p c", p=P))
            neg = kept([P, n_tiles], F32, "neg_level")
            nc.vector.tensor_scalar_mul(neg[:], level_sb[:], -1.0)
            return codes, neg

        def scores(h):
            cols = slice(h * HALF, (h + 1) * HALF)
            for c in range(n_tiles):
                acc = psum.tile([P, BANK], F32, name="acc")
                steps = []
                for g in range(groups):
                    steps.append((w4_codes[:, g, c * P : (c + 1) * P], scale_rows[:, g, c * P : (c + 1) * P], e_q[g, h][0][:], e_q[g, h][1][:]))
                for g in range(groups):
                    w_cols = slice(g * N + c * P, g * N + (c + 1) * P)
                    steps.append((w3_codes[:, w_cols], w3_sc[:, w_cols], x_q[g, h][0][:], x_q[g, h][1][:]))
                steps = [steps[2], steps[0], steps[1], steps[3]]
                for i, (lhsT, lhsT_scale, rhs, rhs_scale) in enumerate(steps):
                    nc.tensor.matmul_mx(
                        out=acc[:, 0:HALF],
                        lhsT=lhsT.bitcast(FP8X4),
                        lhsT_scale=lhsT_scale,
                        rhs=rhs.bitcast(FP8X4),
                        rhs_scale=rhs_scale,
                        start=(i == 0),
                        stop=(i == len(steps) - 1),
                    )
                res = kept([P, HALF], F32, "res%d%d" % (h, c))
                if h == 1 and c == 1:
                    nc.vector.tensor_scalar(res[:], acc[:, 0:HALF], -1.0, neg_level[:, c : c + 1], ALU.mult, ALU.add)
                else:
                    nc.scalar.activation(res[:], acc[:, 0:HALF], ACT.Identity, bias=neg_level[:, c : c + 1], scale=-1.0)
                nc.sync.dma_start(out=out[c * P : (c + 1) * P, cols], in_=res[:])

        def last_halves(rows):
            for h in range(PAIRS // HALF):
                half = kept([P, PACK, HALF], F32, "up1_half")
                entries = pos1_sb[:, h * HALF // 16 : (h + 1) * HALF // 16]
                for t in range(PACK):
                    nc.vector.tensor_copy(half[:, t, :], rows[t][:].indirect(entries))
                maxima(1, h, half[:])
                scores(h)

        quantize_w1(0, 0)
        deal_w2(1, "tab1")
        down_first()
        quantize_w1(1, 0)
        for t in range(PACK):
            down_slice(1, t)
        quantize_w1(0, 1)
        for t in range(2):
            up_slice(t)
        quantize_w1(1, 1)
        up_slice(2)
        up_slice(3)
        w4_codes, neg_level = load_last()
        cast_w3(0, True)
        maxima0()
        rows1 = [rows_of(w1_slice, b1_sb, 1, t) for t in range(PACK)]
        cast_w3(1, True)
        quantize_w3()
        squares(0, 0)
        squares(1, 0)
        squares(0, 1)
        squares(1, 1)
        last_halves(rows1)
